import numpy as np
import ml_dtypes


def mxq(x, axis, fmt="e4m3"):
    dtype, down = {"e4m3": (ml_dtypes.float8_e4m3fn, 7), "e5m2": (ml_dtypes.float8_e5m2, 14)}[fmt]
    v = np.moveaxis(np.asarray(x, np.float32).astype(ml_dtypes.bfloat16).astype(np.float64), axis, -1)
    blocks = v.reshape(v.shape[:-1] + (-1, 32))
    amax = np.abs(blocks).max(-1, keepdims=True)
    byte = np.maximum(np.where(amax > 0, np.frexp(amax)[1] - 1 + 127, 0) - down, 1)
    scale = np.exp2(byte - 127.0)
    codes = (blocks / scale).astype(np.float32).astype(dtype).astype(np.float64)
    return np.moveaxis((codes * scale).reshape(v.shape), -1, axis)


WIDE = False


def mx_kscale(k):
    if not WIDE:
        return np.ones(k)
    levels = np.array([10, -10, 5, -5, 0])
    if k % 512:
        return np.exp2(np.random.permutation(np.resize(levels, k // 32))).repeat(32)
    a = np.empty((k // 512, 16))
    for p in range(k // 512):
        a[p, :8] = np.random.permutation(np.resize(levels, 8))
        for g in range(8):
            far = levels[np.abs(levels - a[p, g]) >= 10]
            a[p, g + 8] = far[np.random.randint(len(far))]
    return np.exp2(a.ravel()).repeat(32)


def f64(x):
    return np.asarray(x).astype(np.float64)


def striped(idx):
    return np.tile(idx.reshape(-1, 16).T, (8, 1)).astype(np.uint16)


def unstriped(offs):
    return offs[:16].T.reshape(-1).astype(np.int64)


E2M1 = np.array([0.0, 0.5, 1.0, 1.5, 2.0, 3.0, 4.0, 6.0, -0.0, -0.5, -1.0, -1.5, -2.0, -3.0, -4.0, -6.0])


def pack_weight(w, fmt):
    k, n = w.shape
    w = f64(np.asarray(w, np.float32).astype(ml_dtypes.bfloat16)).reshape(k // 32, 32, n)
    amax = np.abs(w).max(1)
    if fmt == "e4m3":
        byte = np.frexp(amax)[1] - 1 + 127 - 7
    else:
        mant, ex = np.frexp(amax / 6.0)
        byte = np.where(mant > 0.5, ex, ex - 1) + 127
    byte = np.clip(np.where(amax > 0, byte, 1), 1, 254)
    scaled = (w * np.exp2(127.0 - byte)[:, None, :]).reshape(k, n).astype(np.float32)
    by_word = np.ascontiguousarray(scaled.reshape(k // 512, 128, 4, n).transpose(0, 1, 3, 2))
    if fmt == "e4m3":
        words = by_word.astype(ml_dtypes.float8_e4m3fn).view(np.uint8)
    else:
        c = by_word.astype(ml_dtypes.float4_e2m1fn).view(np.uint8) & 0xF
        words = (c[..., 0::2] | (c[..., 1::2] << 4)).reshape(k // 512, 128, 2 * n)
    return np.ascontiguousarray(words), np.ascontiguousarray(byte.astype(np.uint8).reshape(k // 512, 16, n))


def unpack_weight(words, scales, fmt):
    g, _, n = scales.shape
    words = np.ascontiguousarray(words).reshape(g, 128, n, -1)
    if fmt == "e4m3":
        vals = words.view(ml_dtypes.float8_e4m3fn).astype(np.float64)
    else:
        nib = np.empty((g, 128, n, 4), np.uint8)
        nib[..., 0::2] = words & 0xF
        nib[..., 1::2] = words >> 4
        vals = E2M1[nib]
    vals = vals * np.repeat(np.exp2(scales.astype(np.float64) - 127.0), 8, axis=1)[..., None]
    return vals.transpose(0, 1, 3, 2).reshape(g * 512, n)


def gelu(v):
    return 0.5 * v * (1.0 + np.tanh(np.sqrt(2.0 / np.pi) * (v + 0.044715 * v**3)))


K, K2, T, T2, S, P, H, N = 1024, 512, 4096, 2048, 1024, 512, 1024, 512

def setup_inputs():
    n = np.random.standard_normal
    s, s2, u = mx_kscale(K)[:, None], mx_kscale(K2)[:, None], mx_kscale(H)[:, None]
    d = {}
    d["tab_words"], d["tab_scales"] = pack_weight(n((K, T)) * s, "e4m3")
    d["offs"] = striped(np.random.permutation(T)[:S])
    d["tab2_words"], d["tab2_scales"] = pack_weight(n((K2, T2)) * s2, "e4m3")
    d["offs2"] = striped(np.random.permutation(T2)[:P])
    d["pos1"] = striped(np.random.permutation(S)[:P])
    d["w1_words"], d["w1_scales"] = pack_weight(n((K, H)) / K ** 0.5 / s * u.T, "e2m1")
    d["w2"] = (n((K2, H)) / K2 ** 0.5 / s2 * u.T).astype(np.float32)
    d["w3"] = (n((K2, H)) / K2 ** 0.5 / s2 * u.T).astype(np.float32)
    d["wgs"] = np.exp(0.3 * n((128, P))).astype(np.float32)
    d["w4_words"], d["w4_scales"] = pack_weight(n((H, N)) / H ** 0.5 / u, "e4m3")
    d["pat"] = n((N, S)).astype(np.float32)
    return d

def reference(tab_words, tab_scales, offs, tab2_words, tab2_scales, offs2, pos1,
              w1_words, w1_scales, w2, w3, wgs, w4_words, w4_scales, pat):
    v = unpack_weight(tab_words, tab_scales, "e4m3")[:, unstriped(offs)]
    v2 = unpack_weight(tab2_words, tab2_scales, "e4m3")[:, unstriped(offs2)]
    w1 = unpack_weight(w1_words, w1_scales, "e2m1")
    w4 = unpack_weight(w4_words, w4_scales, "e4m3")
    a = w1.T @ v
    b1 = mxq(f64(w2), 0, "e4m3").T @ v2
    b2 = mxq(f64(w3), 0, "e4m3").T @ v2
    b = np.abs(b1 - b2)
    placed = np.zeros((H, S))
    placed[:, unstriped(pos1)] = np.tile(f64(wgs), (H // 128, 1)) * b
    z = a + placed
    return (w4.T @ mxq(z, 0, "e4m3")) * f64(pat)

@@ -1,0 +1,234 @@
+from contextlib import ExitStack
+
+import concourse.mybir as mybir
+from concourse.masks import make_identity
+
+K, K2, T, T2, S, PL, H, N = 1024, 512, 4096, 2048, 1024, 512, 1024, 512
+FLOPS = 2 * (K * H * S + 2 * K2 * H * PL + H * N * S)
+
+F32 = mybir.dt.float32
+BF16 = mybir.dt.bfloat16
+I32 = mybir.dt.int32
+U32 = mybir.dt.uint32
+U16 = mybir.dt.uint16
+U8 = mybir.dt.uint8
+E4M3 = mybir.dt.float8_e4m3fn_x4
+E2M1 = mybir.dt.float4_e2m1fn_x4
+ACT = mybir.ActivationFunctionType
+MULT = mybir.AluOpType.mult
+
+P = 128
+BANK = 512
+QW = 256
+
+
+def tile_list_parquet_board_matching_kernel(
+    tc, tab_words, tab_scales, offs, tab2_words, tab2_scales, offs2, pos1,
+    w1_words, w1_scales, w2, w3, wgs, w4_words, w4_scales, pat, out,
+):
+    nc = tc.nc
+    with ExitStack() as ctx:
+        keep = ctx.enter_context(tc.tile_pool(name="keep", bufs=1))
+        ring = ctx.enter_context(tc.tile_pool(name="ring", bufs=2))
+        psum = ctx.enter_context(tc.psum_pool(name="psum", bufs=1))
+
+        def kept(name, shape, dtype):
+            return keep.tile(shape, dtype, name=name, align_bytes=64)
+
+        def zeroed_plane(name, shape):
+            plane = kept(name, shape, U8)
+            nc.vector.memset(plane[:].bitcast(I32), 0)
+            return plane
+
+        offs2_sb = keep.tile([P, PL // 16], U16, name="offs2_sb")
+        pos_sb = keep.tile([P, PL // 16], U16, name="pos_sb")
+        offs_sb = keep.tile([P, S // 16], U16, name="offs_sb")
+
+        tab2_s = zeroed_plane("tab2_s", [P, T2])
+        tab_s = zeroed_plane("tab_s", [P, T])
+        w1_s = zeroed_plane("w1_s", [P, 2 * H])
+        w4_s = zeroed_plane("w4_s", [P, 2 * N])
+        v_s1 = zeroed_plane("v_s1", [P, S])
+        ident = kept("ident", [P, P], F32)
+        make_identity(nc, ident[:])
+        pages = []
+        for s in range(2):
+            page = kept(f"page{s}", [P, S], F32)
+            nc.vector.memset(page[:], 0.0)
+            pages.append(page)
+
+        nc.sync.dma_start(offs2_sb[:], offs2)
+        nc.sync.dma_start(pos_sb[:], pos1)
+        nc.sync.dma_start(offs_sb[:], offs)
+        tab2_w = kept("tab2_w", [P, T2], I32)
+        tab2_rows = tab2_words[0].rearrange("p t i -> p (t i)").bitcast(I32)
+        for half in range(2):
+            cols = slice(half * T2 // 2, (half + 1) * T2 // 2)
+            nc.sync.dma_start(tab2_w[:, cols], tab2_rows[:, cols])
+
+        raw = {}
+
+        def load_quarter(c):
+            for i, w in ((1, w3), (0, w2)):
+                raw[c, i] = kept(f"raw{c}_{i}", [P, 4, QW], F32)
+                nc.sync.dma_start(raw[c, i][:], w[:, c * QW : (c + 1) * QW].rearrange("(p j) c -> p j c", j=4))
+
+        load_quarter(0)
+        wgs_sb = kept("wgs_sb", [P, PL], F32)
+        nc.sync.dma_start(wgs_sb[:], wgs)
+        for q in range(4):
+            nc.sync.dma_start(tab2_s[32 * q : 32 * q + 4, :].bitcast(I32), tab2_scales[0, 4 * q : 4 * q + 4, :].bitcast(I32))
+        for q in range(4):
+            nc.sync.dma_start(tab_s[32 * q : 32 * q + 8, :].bitcast(I32), tab_scales[:, 4 * q : 4 * q + 4, :].bitcast(I32))
+        load_quarter(1)
+        load_quarter(2)
+        w1_w = kept("w1_w", [P, 2, 2 * H], U8)
+        nc.sync.dma_start(w1_w[:].bitcast(I32), w1_words.rearrange("a p c -> p a c").bitcast(I32))
+        for q in range(4):
+            nc.sync.dma_start(
+                w1_s[32 * q : 32 * q + 4, :].bitcast(I32).rearrange("r (a c) -> r a c", a=2),
+                w1_scales[:, 4 * q : 4 * q + 4, :].rearrange("a r c -> r a c").bitcast(I32),
+            )
+        tab_w = []
+        for a in range(2):
+            tab_w.append(keep.tile([P, T], I32, name=f"tab_w{a}", tag=f"tab_w{a}", align_bytes=64))
+            nc.sync.dma_start(tab_w[a][:], tab_words[a].rearrange("p t i -> p (t i)").bitcast(I32))
+        load_quarter(3)
+        w4_w = kept("w4_w", [P, 2, N], I32)
+        nc.sync.dma_start(w4_w[:], w4_words.rearrange("a p c i -> p a (c i)").bitcast(I32))
+        for q in range(4):
+            nc.sync.dma_start(
+                w4_s[32 * q : 32 * q + 4, :].bitcast(I32).rearrange("r (a c) -> r a c", a=2),
+                w4_scales[:, 4 * q : 4 * q + 4, :].rearrange("a r c -> r a c").bitcast(I32),
+            )
+        pat_sb = kept("pat_sb", [P, N // P, S], F32)
+        nc.sync.dma_start(pat_sb[:], pat.rearrange("(t p) j -> p t j", p=P))
+
+        v2_w = kept("v2_w", [P, PL], U32)
+        v2_s = kept("v2_s", [P, PL], U8)
+        nc.vector.tensor_copy(v2_w[:], tab2_w[:].bitcast(U32).indirect(offs2_sb[:]))
+        nc.vector.tensor_copy(v2_s[:], tab2_s[:].indirect(offs2_sb[:]))
+
+        b_abs = {}
+
+        def place_quarter(c):
+            grouped = ring.tile([P, 2, QW, 4], BF16, name="w_grouped", align_bytes=64)
+            for i, sign in enumerate((1.0, -1.0)):
+                dst = grouped[:, i].rearrange("p (c i) t -> p c t i", i=4)
+                src = raw[c, i][:].rearrange("p t (c i) -> p c t i", i=4)
+                if c == 0 and i == 0:
+                    nc.vector.tensor_copy(dst, src)
+                else:
+                    nc.scalar.activation(dst, src, ACT.Copy, scale=sign)
+            codes = kept(f"w_codes{c}", [P, 2 * QW], U32)
+            scales = kept(f"w_scales{c}", [P, 2 * QW], U8)
+            nc.vector.quantize_mx(out=codes[:].bitcast(E4M3), scales=scales[:], in_=grouped[:].rearrange("p i c t -> p (i c t)"))
+            for s in range(2 * c, 2 * c + 2):
+                diff = psum.tile([P, PL], F32, name="diff", tag="side", bufs=2)
+                for i in range(2):
+                    cols = slice(i * QW + (s % 2) * P, i * QW + (s % 2 + 1) * P)
+                    nc.tensor.matmul_mx(
+                        out=diff[:], lhsT=codes[:, cols].bitcast(E4M3), lhsT_scale=scales[:, cols],
+                        rhs=v2_w[:].bitcast(E4M3), rhs_scale=v2_s[:], start=(i == 0), stop=(i == 1),
+                    )
+                b_abs[s] = kept(f"b_abs{s}", [P, PL], F32)
+                nc.scalar.activation(b_abs[s][:], diff[:], ACT.Abs)
+
+        def scatter(s):
+            nc.vector.tensor_tensor(pages[s % 3][:].indirect(pos_sb[:]), b_abs[s][:], wgs_sb[:], MULT)
+
+        place_quarter(0)
+        v_s0 = kept("v_s0", [P, S], U8)
+        nc.vector.tensor_copy(v_s0[:], tab_s[:].indirect(offs_sb[:]))
+        nc.sync.dma_start(v_s1[0 : P - 4, :].bitcast(I32), v_s0[4:P, :].bitcast(I32))
+        v_s = (v_s0, v_s1)
+        scatter(0)
+        scatter(1)
+        place_quarter(1)
+        place_quarter(2)
+        v_w = [kept(f"v_w{a}", [P, S], U32) for a in range(2)]
+        for a in range(2):
+            nc.vector.tensor_copy(v_w[a][:], tab_w[a][:].bitcast(U32).indirect(offs_sb[:]))
+        last_page = keep.tile([P, S], F32, name="page2", tag="tab_w1", align_bytes=64)
+        nc.vector.memset(last_page[:], 0.0)
+        pages.append(last_page)
+        scatter(2)
+        place_quarter(3)
+
+        z_t = {(g, h): kept(f"z_t{g}_{h}", [P, 4, BANK], BF16) for g in range(2) for h in range(2)}
+
+        def add_slice(s):
+            g, quarter = divmod(s, 4)
+            totals = []
+            for h in range(2):
+                cols = slice(h * BANK, (h + 1) * BANK)
+                acc = psum.tile([P, BANK], F32, name="acc", tag="acc", bufs=3)
+                for a in range(2):
+                    nc.tensor.matmul_mx(
+                        out=acc[:],
+                        lhsT=w1_w[:, a, 2 * s * P : 2 * (s + 1) * P].bitcast(E2M1),
+                        lhsT_scale=w1_s[:, a * H + s * P : a * H + (s + 1) * P],
+                        rhs=v_w[a][:, cols].bitcast(E4M3), rhs_scale=v_s[a][:, cols],
+                        start=(a == 0), stop=(a == 1),
+                    )
+                a_sb = ring.tile([P, BANK], F32, name="a_sb", tag="a_sb", bufs=4)
+                nc.scalar.copy(a_sb[:], acc[:])
+                total = psum.tile([P, 4, P], F32, name="total", tag="total", bufs=3)
+                totals.append((total, a_sb))
+            for total, a_sb in totals:
+                for jb in range(4):
+                    nc.tensor.matmul(total[:, jb, :], a_sb[:, jb * P : (jb + 1) * P], ident[:], start=(jb == 0), stop=False, is_transpose=True)
+            for h, (total, a_sb) in enumerate(totals):
+                for jb in range(4):
+                    place = h * BANK + jb * P
+                    nc.tensor.matmul(total[:, jb, :], pages[s % 3][:, place : place + P], ident[:], start=False, stop=(jb == 3), is_transpose=True)
+                dst = z_t[g, h][:].rearrange("j b (u p e) -> j b u p e", u=2, e=2)[:, :, :, 32 * quarter : 32 * quarter + 32, :]
+                src = total[:].rearrange("j b (p u e) -> j b u p e", u=2, e=2)
+                if s == 7 and h == 1:
+                    nc.vector.tensor_copy(dst, src)
+                else:
+                    nc.scalar.copy(dst, src)
+            if s + 3 < H // P:
+                scatter(s + 3)
+
+        z_codes, z_scales = {}, {}
+
+        def quantise_pass(g):
+            for h in range(2):
+                words = z_t[g, h][:].bitcast(F32)
+                grouped = ring.tile([P, 4 * BANK], BF16, name="z_grouped", align_bytes=64)
+                for pair in range(2):
+                    turned = psum.tile([P, 2, 2, P], F32, name="turned", tag="side", bufs=2)
+                    for b in range(2):
+                        for u in range(2):
+                            nc.tensor.transpose(turned[:, b, u, :], words[:, 2 * pair + b, u * P : (u + 1) * P], ident[:])
+                    dst = grouped[:].bitcast(F32)[:, pair * BANK : (pair + 1) * BANK].rearrange("p (b j u) -> p b j u", b=2, u=2)
+                    src = turned[:].rearrange("p b u j -> p b j u")
+                    if g == 1 and pair == 1:
+                        nc.vector.tensor_copy(dst, src)
+                    else:
+                        nc.scalar.copy(dst, src)
+                z_codes[g, h] = kept(f"z_codes{g}_{h}", [P, BANK], U32)
+                z_scales[g, h] = kept(f"z_scales{g}_{h}", [P, BANK], U8)
+                nc.vector.quantize_mx(out=z_codes[g, h][:].bitcast(E4M3), scales=z_scales[g, h][:], in_=grouped[:])
+
+        for g in range(2):
+            for s in range(4 * g, 4 * g + 4):
+                add_slice(s)
+            quantise_pass(g)
+
+        for h in range(2):
+            cols = slice(h * BANK, (h + 1) * BANK)
+            for t in range(N // P):
+                acc = psum.tile([P, BANK], F32, name="acc", tag="acc", bufs=3)
+                for g in range(2):
+                    nc.tensor.matmul_mx(
+                        out=acc[:],
+                        lhsT=w4_w[:, g, t * P : (t + 1) * P].bitcast(E4M3),
+                        lhsT_scale=w4_s[:, g * N + t * P : g * N + (t + 1) * P],
+                        rhs=z_codes[g, h][:].bitcast(E4M3), rhs_scale=z_scales[g, h][:],
+                        start=(g == 0), stop=(g == 1),
+                    )
+                result = ring.tile([P, BANK], F32, name="result", tag="result", bufs=4)
+                nc.vector.tensor_tensor(result[:], acc[:], pat_sb[:, t, cols], MULT)
+                nc.sync.dma_start(out[t * P : (t + 1) * P, cols], result[:])

@@ -16,10 +16,14 @@ E4M3 = mybir.dt.float8_e4m3fn_x4
 E2M1 = mybir.dt.float4_e2m1fn_x4
 ACT = mybir.ActivationFunctionType
 MULT = mybir.AluOpType.mult
+ADD = mybir.AluOpType.add
 
 P = 128
 BANK = 512
 QW = 256
+PAGES = 5
+HELD = {2: 0, 3: 4 * T, 4: 4 * T + 4 * PL, 7: 8 * T + 2 * PL}
+VECTOR_ADDS = 2
 
 
 def tile_list_parquet_board_matching_kernel(
@@ -29,42 +33,36 @@ def tile_list_parquet_board_matching_kernel(
     nc = tc.nc
     with ExitStack() as ctx:
         keep = ctx.enter_context(tc.tile_pool(name="keep", bufs=1))
+        shared = ctx.enter_context(tc.tile_pool(name="shared", bufs=1))
         ring = ctx.enter_context(tc.tile_pool(name="ring", bufs=2))
         psum = ctx.enter_context(tc.psum_pool(name="psum", bufs=1))
 
         def kept(name, shape, dtype):
             return keep.tile(shape, dtype, name=name, align_bytes=64)
 
-        def zeroed_plane(name, shape):
+        def zeroed_plane(name, shape, engine):
             plane = kept(name, shape, U8)
-            nc.vector.memset(plane[:].bitcast(I32), 0)
+            engine.memset(plane[:].bitcast(I32), 0)
             return plane
 
         offs2_sb = keep.tile([P, PL // 16], U16, name="offs2_sb")
         pos_sb = keep.tile([P, PL // 16], U16, name="pos_sb")
         offs_sb = keep.tile([P, S // 16], U16, name="offs_sb")
 
-        tab2_s = zeroed_plane("tab2_s", [P, T2])
-        tab_s = zeroed_plane("tab_s", [P, T])
-        w1_s = zeroed_plane("w1_s", [P, 2 * H])
-        w4_s = zeroed_plane("w4_s", [P, 2 * N])
-        v_s1 = zeroed_plane("v_s1", [P, S])
+        tab2_s = zeroed_plane("tab2_s", [P, T2], nc.vector)
+        tab_s = zeroed_plane("tab_s", [P, T], nc.vector)
+        w1_s = zeroed_plane("w1_s", [P, 2 * H], nc.gpsimd)
+        w4_s = zeroed_plane("w4_s", [P, 2 * N], nc.gpsimd)
+        v_s1 = zeroed_plane("v_s1", [P, S], nc.gpsimd)
         ident = kept("ident", [P, P], F32)
         make_identity(nc, ident[:])
+        ident_bf = kept("ident_bf", [P, P], BF16)
+        make_identity(nc, ident_bf[:])
         pages = []
-        for s in range(2):
+        for s in range(PAGES):
             page = kept(f"page{s}", [P, S], F32)
-            nc.vector.memset(page[:], 0.0)
+            (nc.vector if s < 2 else nc.gpsimd).memset(page[:], 0.0)
             pages.append(page)
-
-        nc.sync.dma_start(offs2_sb[:], offs2)
-        nc.sync.dma_start(pos_sb[:], pos1)
-        nc.sync.dma_start(offs_sb[:], offs)
-        tab2_w = kept("tab2_w", [P, T2], I32)
-        tab2_rows = tab2_words[0].rearrange("p t i -> p (t i)").bitcast(I32)
-        for half in range(2):
-            cols = slice(half * T2 // 2, (half + 1) * T2 // 2)
-            nc.sync.dma_start(tab2_w[:, cols], tab2_rows[:, cols])
 
         raw = {}
 
@@ -73,43 +71,26 @@ def tile_list_parquet_board_matching_kernel(
                 raw[c, i] = kept(f"raw{c}_{i}", [P, 4, QW], F32)
                 nc.sync.dma_start(raw[c, i][:], w[:, c * QW : (c + 1) * QW].rearrange("(p j) c -> p j c", j=4))
 
+        nc.sync.dma_start(offs2_sb[:], offs2)
+        tab2_w = kept("tab2_w", [P, T2], I32)
+        nc.sync.dma_start(tab2_w[:], tab2_words[0].rearrange("p t i -> p (t i)").bitcast(I32))
+        for q in range(4):
+            nc.scalar.dma_start(tab2_s[32 * q : 32 * q + 4, :].bitcast(I32), tab2_scales[0, 4 * q : 4 * q + 4, :].bitcast(I32))
         load_quarter(0)
+        nc.sync.dma_start(offs_sb[:], offs)
+        for q in range(4):
+            queue = nc.scalar if q < 2 else nc.sync
+            queue.dma_start(tab_s[32 * q : 32 * q + 8, :].bitcast(I32), tab_scales[:, 4 * q : 4 * q + 4, :].bitcast(I32))
         wgs_sb = kept("wgs_sb", [P, PL], F32)
         nc.sync.dma_start(wgs_sb[:], wgs)
-        for q in range(4):
-            nc.sync.dma_start(tab2_s[32 * q : 32 * q + 4, :].bitcast(I32), tab2_scales[0, 4 * q : 4 * q + 4, :].bitcast(I32))
-        for q in range(4):
-            nc.sync.dma_start(tab_s[32 * q : 32 * q + 8, :].bitcast(I32), tab_scales[:, 4 * q : 4 * q + 4, :].bitcast(I32))
-        load_quarter(1)
-        load_quarter(2)
-        w1_w = kept("w1_w", [P, 2, 2 * H], U8)
-        nc.sync.dma_start(w1_w[:].bitcast(I32), w1_words.rearrange("a p c -> p a c").bitcast(I32))
-        for q in range(4):
-            nc.sync.dma_start(
-                w1_s[32 * q : 32 * q + 4, :].bitcast(I32).rearrange("r (a c) -> r a c", a=2),
-                w1_scales[:, 4 * q : 4 * q + 4, :].rearrange("a r c -> r a c").bitcast(I32),
-            )
-        tab_w = []
-        for a in range(2):
-            tab_w.append(keep.tile([P, T], I32, name=f"tab_w{a}", tag=f"tab_w{a}", align_bytes=64))
-            nc.sync.dma_start(tab_w[a][:], tab_words[a].rearrange("p t i -> p (t i)").bitcast(I32))
-        load_quarter(3)
-        w4_w = kept("w4_w", [P, 2, N], I32)
-        nc.sync.dma_start(w4_w[:], w4_words.rearrange("a p c i -> p a (c i)").bitcast(I32))
-        for q in range(4):
-            nc.sync.dma_start(
-                w4_s[32 * q : 32 * q + 4, :].bitcast(I32).rearrange("r (a c) -> r a c", a=2),
-                w4_scales[:, 4 * q : 4 * q + 4, :].rearrange("a r c -> r a c").bitcast(I32),
-            )
-        pat_sb = kept("pat_sb", [P, N // P, S], F32)
-        nc.sync.dma_start(pat_sb[:], pat.rearrange("(t p) j -> p t j", p=P))
+        nc.sync.dma_start(pos_sb[:], pos1)
 
         v2_w = kept("v2_w", [P, PL], U32)
         v2_s = kept("v2_s", [P, PL], U8)
         nc.vector.tensor_copy(v2_w[:], tab2_w[:].bitcast(U32).indirect(offs2_sb[:]))
         nc.vector.tensor_copy(v2_s[:], tab2_s[:].indirect(offs2_sb[:]))
 
-        b_abs = {}
+        b_abs, w_mx = {}, {}
 
         def place_quarter(c):
             grouped = ring.tile([P, 2, QW, 4], BF16, name="w_grouped", align_bytes=64)
@@ -123,43 +104,77 @@ def tile_list_parquet_board_matching_kernel(
             codes = kept(f"w_codes{c}", [P, 2 * QW], U32)
             scales = kept(f"w_scales{c}", [P, 2 * QW], U8)
             nc.vector.quantize_mx(out=codes[:].bitcast(E4M3), scales=scales[:], in_=grouped[:].rearrange("p i c t -> p (i c t)"))
-            for s in range(2 * c, 2 * c + 2):
-                diff = psum.tile([P, PL], F32, name="diff", tag="side", bufs=2)
+            w_mx[c] = (codes, scales)
+
+        def differences(slices):
+            for s in slices:
+                codes, scales = w_mx[s // 2]
+                diff = psum.tile([P, PL], F32, name="diff", tag="side" if s < 5 else "total", bufs=2 if s < 5 else 3)
                 for i in range(2):
                     cols = slice(i * QW + (s % 2) * P, i * QW + (s % 2 + 1) * P)
                     nc.tensor.matmul_mx(
                         out=diff[:], lhsT=codes[:, cols].bitcast(E4M3), lhsT_scale=scales[:, cols],
                         rhs=v2_w[:].bitcast(E4M3), rhs_scale=v2_s[:], start=(i == 0), stop=(i == 1),
                     )
-                b_abs[s] = kept(f"b_abs{s}", [P, PL], F32)
+                if s in HELD:
+                    b_abs[s] = shared.tile([P, PL], F32, name=f"b_abs{s}", align_bytes=64, offset=HELD[s])
+                else:
+                    b_abs[s] = kept(f"b_abs{s}", [P, PL], F32)
                 nc.scalar.activation(b_abs[s][:], diff[:], ACT.Abs)
 
         def scatter(s):
-            nc.vector.tensor_tensor(pages[s % 3][:].indirect(pos_sb[:]), b_abs[s][:], wgs_sb[:], MULT)
+            nc.vector.tensor_tensor(pages[s % PAGES][:].indirect(pos_sb[:]), b_abs[s][:], wgs_sb[:], MULT)
 
         place_quarter(0)
+        differences((0, 1))
         v_s0 = kept("v_s0", [P, S], U8)
         nc.vector.tensor_copy(v_s0[:], tab_s[:].indirect(offs_sb[:]))
-        nc.sync.dma_start(v_s1[0 : P - 4, :].bitcast(I32), v_s0[4:P, :].bitcast(I32))
+        nc.gpsimd.dma_start(v_s1[0 : P - 4, :].bitcast(I32), v_s0[4:P, :].bitcast(I32))
         v_s = (v_s0, v_s1)
+        load_quarter(1)
+        w1_w = kept("w1_w", [P, 2, 2 * H], U8)
+        nc.sync.dma_start(w1_w[:].bitcast(I32), w1_words.rearrange("a p c -> p a c").bitcast(I32))
+        for q in range(4):
+            nc.sync.dma_start(
+                w1_s[32 * q : 32 * q + 4, :].bitcast(I32).rearrange("r (a c) -> r a c", a=2),
+                w1_scales[:, 4 * q : 4 * q + 4, :].rearrange("a r c -> r a c").bitcast(I32),
+            )
+        tab_w = []
+        for a in range(2):
+            tab_w.append(shared.tile([P, T], I32, name=f"tab_w{a}", align_bytes=64, offset=a * 4 * T))
+        nc.sync.dma_start(tab_w[0][:], tab_words[0].rearrange("p t i -> p (t i)").bitcast(I32))
+        for c in range(2, 4):
+            load_quarter(c)
+        nc.sync.dma_start(tab_w[1][:], tab_words[1].rearrange("p t i -> p (t i)").bitcast(I32))
+        w4_w = kept("w4_w", [P, 2, N], I32)
+        nc.sync.dma_start(w4_w[:], w4_words.rearrange("a p c i -> p a (c i)").bitcast(I32))
+        for q in range(4):
+            nc.sync.dma_start(
+                w4_s[32 * q : 32 * q + 4, :].bitcast(I32).rearrange("r (a c) -> r a c", a=2),
+                w4_scales[:, 4 * q : 4 * q + 4, :].rearrange("a r c -> r a c").bitcast(I32),
+            )
+        pat_sb = kept("pat_sb", [P, N // P, S], F32)
+        nc.sync.dma_start(pat_sb[:], pat.rearrange("(t p) j -> p t j", p=P))
+
         scatter(0)
         scatter(1)
-        place_quarter(1)
-        place_quarter(2)
         v_w = [kept(f"v_w{a}", [P, S], U32) for a in range(2)]
-        for a in range(2):
-            nc.vector.tensor_copy(v_w[a][:], tab_w[a][:].bitcast(U32).indirect(offs_sb[:]))
-        last_page = keep.tile([P, S], F32, name="page2", tag="tab_w1", align_bytes=64)
-        nc.vector.memset(last_page[:], 0.0)
-        pages.append(last_page)
+        place_quarter(1)
+        nc.vector.tensor_copy(v_w[0][:], tab_w[0][:].bitcast(U32).indirect(offs_sb[:]))
+        differences((2,))
         scatter(2)
+        place_quarter(2)
         place_quarter(3)
+        nc.vector.tensor_copy(v_w[1][:], tab_w[1][:].bitcast(U32).indirect(offs_sb[:]))
+        differences((3, 4, 5, 6, 7))
+        scatter(3)
+        scatter(4)
 
         z_t = {(g, h): kept(f"z_t{g}_{h}", [P, 4, BANK], BF16) for g in range(2) for h in range(2)}
 
-        def add_slice(s):
-            g, quarter = divmod(s, 4)
-            totals = []
+        a_parts = {}
+
+        def features(s):
             for h in range(2):
                 cols = slice(h * BANK, (h + 1) * BANK)
                 acc = psum.tile([P, BANK], F32, name="acc", tag="acc", bufs=3)
@@ -171,32 +186,52 @@ def tile_list_parquet_board_matching_kernel(
                         rhs=v_w[a][:, cols].bitcast(E4M3), rhs_scale=v_s[a][:, cols],
                         start=(a == 0), stop=(a == 1),
                     )
-                a_sb = ring.tile([P, BANK], F32, name="a_sb", tag="a_sb", bufs=4)
+                if s >= H // P - VECTOR_ADDS:
+                    a_parts[s, h] = acc
+                    continue
+                a_sb = ring.tile([P, BANK], F32, name="a_sb", tag="a_sb", bufs=6)
                 nc.scalar.copy(a_sb[:], acc[:])
-                total = psum.tile([P, 4, P], F32, name="total", tag="total", bufs=3)
-                totals.append((total, a_sb))
+                a_parts[s, h] = a_sb
+
+        def add_slice(s):
+            g, quarter = divmod(s, 4)
+            totals = [(psum.tile([P, 4, P], F32, name="total", tag="total", bufs=3), a_parts[s, h]) for h in range(2)]
             for total, a_sb in totals:
                 for jb in range(4):
                     nc.tensor.matmul(total[:, jb, :], a_sb[:, jb * P : (jb + 1) * P], ident[:], start=(jb == 0), stop=False, is_transpose=True)
             for h, (total, a_sb) in enumerate(totals):
                 for jb in range(4):
                     place = h * BANK + jb * P
-                    nc.tensor.matmul(total[:, jb, :], pages[s % 3][:, place : place + P], ident[:], start=False, stop=(jb == 3), is_transpose=True)
+                    nc.tensor.matmul(total[:, jb, :], pages[s % PAGES][:, place : place + P], ident[:], start=False, stop=(jb == 3), is_transpose=True)
                 dst = z_t[g, h][:].rearrange("j b (u p e) -> j b u p e", u=2, e=2)[:, :, :, 32 * quarter : 32 * quarter + 32, :]
                 src = total[:].rearrange("j b (p u e) -> j b u p e", u=2, e=2)
-                if s == 7 and h == 1:
-                    nc.vector.tensor_copy(dst, src)
-                else:
-                    nc.scalar.copy(dst, src)
-            if s + 3 < H // P:
-                scatter(s + 3)
+                nc.scalar.copy(dst, src)
+            if s + PAGES < H // P:
+                scatter(s + PAGES)
+
+        def add_slice_on_vector(s):
+            g, quarter = divmod(s, 4)
+            features(s)
+            for h in range(2):
+                z_sb = ring.tile([P, BANK], BF16, name="z_sb", tag="z_sb", bufs=4)
+                nc.vector.tensor_tensor(z_sb[:], a_parts[s, h][:], pages[s % PAGES][:, h * BANK : (h + 1) * BANK], ADD)
+                total = psum.tile([P, 4, P], BF16, name="total_bf", tag="total", bufs=3)
+                for jb in range(4):
+                    nc.tensor.transpose(total[:, jb, :], z_sb[:, jb * P : (jb + 1) * P], ident_bf[:])
+                nc.scalar.copy(
+                    z_t[g, h][:].bitcast(F32).rearrange("j b (u p) -> j b u p", u=2)[:, :, :, 32 * quarter : 32 * quarter + 32],
+                    total[:].bitcast(F32).rearrange("j b (p u) -> j b u p", u=2),
+                )
 
         z_codes, z_scales = {}, {}
 
-        def quantise_pass(g):
+        z_grouped = {}
+
+        def regroup_pass(g):
             for h in range(2):
                 words = z_t[g, h][:].bitcast(F32)
-                grouped = ring.tile([P, 4 * BANK], BF16, name="z_grouped", align_bytes=64)
+                grouped = ring.tile([P, 4 * BANK], BF16, name="z_grouped", align_bytes=64, bufs=4)
+                z_grouped[g, h] = grouped
                 for pair in range(2):
                     turned = psum.tile([P, 2, 2, P], F32, name="turned", tag="side", bufs=2)
                     for b in range(2):
@@ -204,18 +239,33 @@ def tile_list_parquet_board_matching_kernel(
                             nc.tensor.transpose(turned[:, b, u, :], words[:, 2 * pair + b, u * P : (u + 1) * P], ident[:])
                     dst = grouped[:].bitcast(F32)[:, pair * BANK : (pair + 1) * BANK].rearrange("p (b j u) -> p b j u", b=2, u=2)
                     src = turned[:].rearrange("p b u j -> p b j u")
-                    if g == 1 and pair == 1:
+                    if g == 1 and pair == 1 and h == 0:
                         nc.vector.tensor_copy(dst, src)
                     else:
                         nc.scalar.copy(dst, src)
-                z_codes[g, h] = kept(f"z_codes{g}_{h}", [P, BANK], U32)
-                z_scales[g, h] = kept(f"z_scales{g}_{h}", [P, BANK], U8)
-                nc.vector.quantize_mx(out=z_codes[g, h][:].bitcast(E4M3), scales=z_scales[g, h][:], in_=grouped[:])
 
-        for g in range(2):
-            for s in range(4 * g, 4 * g + 4):
-                add_slice(s)
-            quantise_pass(g)
+        def quantise_pass(g):
+            for h in range(2):
+                if g == 0:
+                    z_codes[g, h] = shared.tile([P, BANK], U32, name=f"z_codes{g}_{h}", align_bytes=64, offset=HELD[7] + (4 * h - 2) * PL)
+                else:
+                    z_codes[g, h] = kept(f"z_codes{g}_{h}", [P, BANK], U32)
+                z_scales[g, h] = kept(f"z_scales{g}_{h}", [P, BANK], U8)
+                nc.vector.quantize_mx(out=z_codes[g, h][:].bitcast(E4M3), scales=z_scales[g, h][:], in_=z_grouped[g, h][:])
+
+        on_tensor = H // P - VECTOR_ADDS
+        features(0)
+        for s in range(on_tensor):
+            if s + 1 < on_tensor:
+                features(s + 1)
+            add_slice(s)
+            if s == 4:
+                regroup_pass(0)
+        for s in range(on_tensor, H // P):
+            add_slice_on_vector(s)
+        quantise_pass(0)
+        regroup_pass(1)
+        quantise_pass(1)
 
         for h in range(2):
             cols = slice(h * BANK, (h + 1) * BANK)

from contextlib import ExitStack

import concourse.mybir as mybir
from concourse.masks import make_identity

K, K2, T, T2, S, PL, H, N = 1024, 512, 4096, 2048, 1024, 512, 1024, 512
FLOPS = 2 * (K * H * S + 2 * K2 * H * PL + H * N * S)

F32 = mybir.dt.float32
BF16 = mybir.dt.bfloat16
I32 = mybir.dt.int32
U32 = mybir.dt.uint32
U16 = mybir.dt.uint16
U8 = mybir.dt.uint8
E4M3 = mybir.dt.float8_e4m3fn_x4
E2M1 = mybir.dt.float4_e2m1fn_x4
ACT = mybir.ActivationFunctionType
MULT = mybir.AluOpType.mult
ADD = mybir.AluOpType.add

P = 128
BANK = 512
QW = 256
PAGES = 5
HELD = {2: 0, 3: 4 * T, 4: 4 * T + 4 * PL, 7: 8 * T + 2 * PL}
VECTOR_ADDS = 2


def tile_list_parquet_board_matching_kernel(
    tc, tab_words, tab_scales, offs, tab2_words, tab2_scales, offs2, pos1,
    w1_words, w1_scales, w2, w3, wgs, w4_words, w4_scales, pat, out,
):
    nc = tc.nc
    with ExitStack() as ctx:
        keep = ctx.enter_context(tc.tile_pool(name="keep", bufs=1))
        shared = ctx.enter_context(tc.tile_pool(name="shared", bufs=1))
        ring = ctx.enter_context(tc.tile_pool(name="ring", bufs=2))
        psum = ctx.enter_context(tc.psum_pool(name="psum", bufs=1))

        def kept(name, shape, dtype):
            return keep.tile(shape, dtype, name=name, align_bytes=64)

        def zeroed_plane(name, shape, engine):
            plane = kept(name, shape, U8)
            engine.memset(plane[:].bitcast(I32), 0)
            return plane

        offs2_sb = keep.tile([P, PL // 16], U16, name="offs2_sb")
        pos_sb = keep.tile([P, PL // 16], U16, name="pos_sb")
        offs_sb = keep.tile([P, S // 16], U16, name="offs_sb")

        tab2_s = zeroed_plane("tab2_s", [P, T2], nc.vector)
        tab_s = zeroed_plane("tab_s", [P, T], nc.vector)
        w1_s = zeroed_plane("w1_s", [P, 2 * H], nc.gpsimd)
        w4_s = zeroed_plane("w4_s", [P, 2 * N], nc.gpsimd)
        v_s1 = zeroed_plane("v_s1", [P, S], nc.gpsimd)
        ident = kept("ident", [P, P], F32)
        make_identity(nc, ident[:])
        ident_bf = kept("ident_bf", [P, P], BF16)
        make_identity(nc, ident_bf[:])
        pages = []
        for s in range(PAGES):
            page = kept(f"page{s}", [P, S], F32)
            (nc.vector if s < 2 else nc.gpsimd).memset(page[:], 0.0)
            pages.append(page)

        raw = {}

        def load_quarter(c):
            for i, w in ((1, w3), (0, w2)):
                raw[c, i] = kept(f"raw{c}_{i}", [P, 4, QW], F32)
                nc.sync.dma_start(raw[c, i][:], w[:, c * QW : (c + 1) * QW].rearrange("(p j) c -> p j c", j=4))

        nc.sync.dma_start(offs2_sb[:], offs2)
        tab2_w = kept("tab2_w", [P, T2], I32)
        nc.sync.dma_start(tab2_w[:], tab2_words[0].rearrange("p t i -> p (t i)").bitcast(I32))
        for q in range(4):
            nc.scalar.dma_start(tab2_s[32 * q : 32 * q + 4, :].bitcast(I32), tab2_scales[0, 4 * q : 4 * q + 4, :].bitcast(I32))
        load_quarter(0)
        nc.sync.dma_start(offs_sb[:], offs)
        for q in range(4):
            queue = nc.scalar if q < 2 else nc.sync
            queue.dma_start(tab_s[32 * q : 32 * q + 8, :].bitcast(I32), tab_scales[:, 4 * q : 4 * q + 4, :].bitcast(I32))
        wgs_sb = kept("wgs_sb", [P, PL], F32)
        nc.sync.dma_start(wgs_sb[:], wgs)
        nc.sync.dma_start(pos_sb[:], pos1)

        v2_w = kept("v2_w", [P, PL], U32)
        v2_s = kept("v2_s", [P, PL], U8)
        nc.vector.tensor_copy(v2_w[:], tab2_w[:].bitcast(U32).indirect(offs2_sb[:]))
        nc.vector.tensor_copy(v2_s[:], tab2_s[:].indirect(offs2_sb[:]))

        b_abs, w_mx = {}, {}

        def place_quarter(c):
            grouped = ring.tile([P, 2, QW, 4], BF16, name="w_grouped", align_bytes=64)
            for i, sign in enumerate((1.0, -1.0)):
                dst = grouped[:, i].rearrange("p (c i) t -> p c t i", i=4)
                src = raw[c, i][:].rearrange("p t (c i) -> p c t i", i=4)
                if c == 0 and i == 0:
                    nc.vector.tensor_copy(dst, src)
                else:
                    nc.scalar.activation(dst, src, ACT.Copy, scale=sign)
            codes = kept(f"w_codes{c}", [P, 2 * QW], U32)
            scales = kept(f"w_scales{c}", [P, 2 * QW], U8)
            nc.vector.quantize_mx(out=codes[:].bitcast(E4M3), scales=scales[:], in_=grouped[:].rearrange("p i c t -> p (i c t)"))
            w_mx[c] = (codes, scales)

        def differences(slices):
            for s in slices:
                codes, scales = w_mx[s // 2]
                diff = psum.tile([P, PL], F32, name="diff", tag="side" if s < 5 else "total", bufs=2 if s < 5 else 3)
                for i in range(2):
                    cols = slice(i * QW + (s % 2) * P, i * QW + (s % 2 + 1) * P)
                    nc.tensor.matmul_mx(
                        out=diff[:], lhsT=codes[:, cols].bitcast(E4M3), lhsT_scale=scales[:, cols],
                        rhs=v2_w[:].bitcast(E4M3), rhs_scale=v2_s[:], start=(i == 0), stop=(i == 1),
                    )
                if s in HELD:
                    b_abs[s] = shared.tile([P, PL], F32, name=f"b_abs{s}", align_bytes=64, offset=HELD[s])
                else:
                    b_abs[s] = kept(f"b_abs{s}", [P, PL], F32)
                nc.scalar.activation(b_abs[s][:], diff[:], ACT.Abs)

        def scatter(s):
            nc.vector.tensor_tensor(pages[s % PAGES][:].indirect(pos_sb[:]), b_abs[s][:], wgs_sb[:], MULT)

        place_quarter(0)
        differences((0, 1))
        v_s0 = kept("v_s0", [P, S], U8)
        nc.vector.tensor_copy(v_s0[:], tab_s[:].indirect(offs_sb[:]))
        nc.gpsimd.dma_start(v_s1[0 : P - 4, :].bitcast(I32), v_s0[4:P, :].bitcast(I32))
        v_s = (v_s0, v_s1)
        load_quarter(1)
        w1_w = kept("w1_w", [P, 2, 2 * H], U8)
        nc.sync.dma_start(w1_w[:].bitcast(I32), w1_words.rearrange("a p c -> p a c").bitcast(I32))
        for q in range(4):
            nc.sync.dma_start(
                w1_s[32 * q : 32 * q + 4, :].bitcast(I32).rearrange("r (a c) -> r a c", a=2),
                w1_scales[:, 4 * q : 4 * q + 4, :].rearrange("a r c -> r a c").bitcast(I32),
            )
        tab_w = []
        for a in range(2):
            tab_w.append(shared.tile([P, T], I32, name=f"tab_w{a}", align_bytes=64, offset=a * 4 * T))
        nc.sync.dma_start(tab_w[0][:], tab_words[0].rearrange("p t i -> p (t i)").bitcast(I32))
        for c in range(2, 4):
            load_quarter(c)
        nc.sync.dma_start(tab_w[1][:], tab_words[1].rearrange("p t i -> p (t i)").bitcast(I32))
        w4_w = kept("w4_w", [P, 2, N], I32)
        nc.sync.dma_start(w4_w[:], w4_words.rearrange("a p c i -> p a (c i)").bitcast(I32))
        for q in range(4):
            nc.sync.dma_start(
                w4_s[32 * q : 32 * q + 4, :].bitcast(I32).rearrange("r (a c) -> r a c", a=2),
                w4_scales[:, 4 * q : 4 * q + 4, :].rearrange("a r c -> r a c").bitcast(I32),
            )
        pat_sb = kept("pat_sb", [P, N // P, S], F32)
        nc.sync.dma_start(pat_sb[:], pat.rearrange("(t p) j -> p t j", p=P))

        scatter(0)
        scatter(1)
        v_w = [kept(f"v_w{a}", [P, S], U32) for a in range(2)]
        place_quarter(1)
        nc.vector.tensor_copy(v_w[0][:], tab_w[0][:].bitcast(U32).indirect(offs_sb[:]))
        differences((2,))
        scatter(2)
        place_quarter(2)
        place_quarter(3)
        nc.vector.tensor_copy(v_w[1][:], tab_w[1][:].bitcast(U32).indirect(offs_sb[:]))
        differences((3, 4, 5, 6, 7))
        scatter(3)
        scatter(4)

        z_t = {(g, h): kept(f"z_t{g}_{h}", [P, 4, BANK], BF16) for g in range(2) for h in range(2)}

        a_parts = {}

        def features(s):
            for h in range(2):
                cols = slice(h * BANK, (h + 1) * BANK)
                acc = psum.tile([P, BANK], F32, name="acc", tag="acc", bufs=3)
                for a in range(2):
                    nc.tensor.matmul_mx(
                        out=acc[:],
                        lhsT=w1_w[:, a, 2 * s * P : 2 * (s + 1) * P].bitcast(E2M1),
                        lhsT_scale=w1_s[:, a * H + s * P : a * H + (s + 1) * P],
                        rhs=v_w[a][:, cols].bitcast(E4M3), rhs_scale=v_s[a][:, cols],
                        start=(a == 0), stop=(a == 1),
                    )
                if s >= H // P - VECTOR_ADDS:
                    a_parts[s, h] = acc
                    continue
                a_sb = ring.tile([P, BANK], F32, name="a_sb", tag="a_sb", bufs=6)
                nc.scalar.copy(a_sb[:], acc[:])
                a_parts[s, h] = a_sb

        def add_slice(s):
            g, quarter = divmod(s, 4)
            totals = [(psum.tile([P, 4, P], F32, name="total", tag="total", bufs=3), a_parts[s, h]) for h in range(2)]
            for total, a_sb in totals:
                for jb in range(4):
                    nc.tensor.matmul(total[:, jb, :], a_sb[:, jb * P : (jb + 1) * P], ident[:], start=(jb == 0), stop=False, is_transpose=True)
            for h, (total, a_sb) in enumerate(totals):
                for jb in range(4):
                    place = h * BANK + jb * P
                    nc.tensor.matmul(total[:, jb, :], pages[s % PAGES][:, place : place + P], ident[:], start=False, stop=(jb == 3), is_transpose=True)
                dst = z_t[g, h][:].rearrange("j b (u p e) -> j b u p e", u=2, e=2)[:, :, :, 32 * quarter : 32 * quarter + 32, :]
                src = total[:].rearrange("j b (p u e) -> j b u p e", u=2, e=2)
                nc.scalar.copy(dst, src)
            if s + PAGES < H // P:
                scatter(s + PAGES)

        def add_slice_on_vector(s):
            g, quarter = divmod(s, 4)
            features(s)
            for h in range(2):
                z_sb = ring.tile([P, BANK], BF16, name="z_sb", tag="z_sb", bufs=4)
                nc.vector.tensor_tensor(z_sb[:], a_parts[s, h][:], pages[s % PAGES][:, h * BANK : (h + 1) * BANK], ADD)
                total = psum.tile([P, 4, P], BF16, name="total_bf", tag="total", bufs=3)
                for jb in range(4):
                    nc.tensor.transpose(total[:, jb, :], z_sb[:, jb * P : (jb + 1) * P], ident_bf[:])
                nc.scalar.copy(
                    z_t[g, h][:].bitcast(F32).rearrange("j b (u p) -> j b u p", u=2)[:, :, :, 32 * quarter : 32 * quarter + 32],
                    total[:].bitcast(F32).rearrange("j b (p u) -> j b u p", u=2),
                )

        z_codes, z_scales = {}, {}

        z_grouped = {}

        def regroup_pass(g):
            for h in range(2):
                words = z_t[g, h][:].bitcast(F32)
                grouped = ring.tile([P, 4 * BANK], BF16, name="z_grouped", align_bytes=64, bufs=4)
                z_grouped[g, h] = grouped
                for pair in range(2):
                    turned = psum.tile([P, 2, 2, P], F32, name="turned", tag="side", bufs=2)
                    for b in range(2):
                        for u in range(2):
                            nc.tensor.transpose(turned[:, b, u, :], words[:, 2 * pair + b, u * P : (u + 1) * P], ident[:])
                    dst = grouped[:].bitcast(F32)[:, pair * BANK : (pair + 1) * BANK].rearrange("p (b j u) -> p b j u", b=2, u=2)
                    src = turned[:].rearrange("p b u j -> p b j u")
                    if g == 1 and pair == 1 and h == 0:
                        nc.vector.tensor_copy(dst, src)
                    else:
                        nc.scalar.copy(dst, src)

        def quantise_pass(g):
            for h in range(2):
                if g == 0:
                    z_codes[g, h] = shared.tile([P, BANK], U32, name=f"z_codes{g}_{h}", align_bytes=64, offset=HELD[7] + (4 * h - 2) * PL)
                else:
                    z_codes[g, h] = kept(f"z_codes{g}_{h}", [P, BANK], U32)
                z_scales[g, h] = kept(f"z_scales{g}_{h}", [P, BANK], U8)
                nc.vector.quantize_mx(out=z_codes[g, h][:].bitcast(E4M3), scales=z_scales[g, h][:], in_=z_grouped[g, h][:])

        on_tensor = H // P - VECTOR_ADDS
        features(0)
        for s in range(on_tensor):
            if s + 1 < on_tensor:
                features(s + 1)
            add_slice(s)
            if s == 4:
                regroup_pass(0)
        for s in range(on_tensor, H // P):
            add_slice_on_vector(s)
        quantise_pass(0)
        regroup_pass(1)
        quantise_pass(1)

        for h in range(2):
            cols = slice(h * BANK, (h + 1) * BANK)
            for t in range(N // P):
                acc = psum.tile([P, BANK], F32, name="acc", tag="acc", bufs=3)
                for g in range(2):
                    nc.tensor.matmul_mx(
                        out=acc[:],
                        lhsT=w4_w[:, g, t * P : (t + 1) * P].bitcast(E4M3),
                        lhsT_scale=w4_s[:, g * N + t * P : g * N + (t + 1) * P],
                        rhs=z_codes[g, h][:].bitcast(E4M3), rhs_scale=z_scales[g, h][:],
                        start=(g == 0), stop=(g == 1),
                    )
                result = ring.tile([P, BANK], F32, name="result", tag="result", bufs=4)
                nc.vector.tensor_tensor(result[:], acc[:], pat_sb[:, t, cols], MULT)
                nc.sync.dma_start(out[t * P : (t + 1) * P, cols], result[:])
